import numpy as np
import ml_dtypes


def mxq(x, axis, fmt="e4m3"):
    dtype, down = {"e4m3": (ml_dtypes.float8_e4m3fn, 7), "e5m2": (ml_dtypes.float8_e5m2, 14)}[fmt]
    v = np.moveaxis(np.asarray(x, np.float32).astype(ml_dtypes.bfloat16).astype(np.float64), axis, -1)
    blocks = v.reshape(v.shape[:-1] + (-1, 32))
    amax = np.abs(blocks).max(-1, keepdims=True)
    byte = np.maximum(np.where(amax > 0, np.frexp(amax)[1] - 1 + 127, 0) - down, 1)
    scale = np.exp2(byte - 127.0)
    codes = (blocks / scale).astype(np.float32).astype(dtype).astype(np.float64)
    return np.moveaxis((codes * scale).reshape(v.shape), -1, axis)


WIDE = False


def mx_kscale(k):
    if not WIDE:
        return np.ones(k)
    levels = np.array([10, -10, 5, -5, 0])
    if k % 512:
        return np.exp2(np.random.permutation(np.resize(levels, k // 32))).repeat(32)
    a = np.empty((k // 512, 16))
    for p in range(k // 512):
        a[p, :8] = np.random.permutation(np.resize(levels, 8))
        for g in range(8):
            far = levels[np.abs(levels - a[p, g]) >= 10]
            a[p, g + 8] = far[np.random.randint(len(far))]
    return np.exp2(a.ravel()).repeat(32)


def f64(x):
    return np.asarray(x).astype(np.float64)


def striped(idx):
    return np.tile(idx.reshape(-1, 16).T, (8, 1)).astype(np.uint16)


def unstriped(offs):
    return offs[:16].T.reshape(-1).astype(np.int64)


def striped8(idx):
    return np.concatenate([x.reshape(-1, 16).T for x in idx]).astype(np.uint16)


def runs(offs, k):
    lists = np.stack([offs[16 * r : 16 * r + 16].T.reshape(-1) for r in range(8)]).astype(np.int64)
    return lists[np.arange(k) % 512 // 64]


def pack_weight(w):
    k, n = w.shape
    w = f64(np.asarray(w, np.float32).astype(ml_dtypes.bfloat16)).reshape(k // 32, 32, n)
    amax = np.abs(w).max(1)
    byte = np.clip(np.where(amax > 0, np.frexp(amax)[1] - 1 + 127 - 7, 1), 1, 254)
    scaled = (w * np.exp2(127.0 - byte)[:, None, :]).reshape(k, n).astype(np.float32)
    words = np.ascontiguousarray(scaled.reshape(k // 512, 128, 4, n).transpose(0, 1, 3, 2)).astype(ml_dtypes.float8_e4m3fn).view(np.uint8)
    return words, np.ascontiguousarray(byte.astype(np.uint8).reshape(k // 512, 16, n))


def unpack_weight(words, scales):
    g, p, n, _ = words.shape
    vals = np.ascontiguousarray(words).view(ml_dtypes.float8_e4m3fn).astype(np.float64) * np.repeat(np.exp2(scales.astype(np.float64) - 127.0), 8, axis=1)[..., None]
    return vals.transpose(0, 1, 3, 2).reshape(g * 512, n)


def relu(v):
    return np.maximum(v, 0.0)


K, T, S, N, G, H = 512, 1024, 256, 512, 2048, 512


def setup_inputs():
    n = np.random.standard_normal
    s = mx_kscale(K)[:, None]
    u = mx_kscale(K)
    packed_xT = pack_weight(n((K, T)) * s)
    packed_dT = pack_weight(n((K, G)) / s)
    return {
        "x_words": packed_xT[0],
        "x_scales": packed_xT[1],
        "d_words": packed_dT[0],
        "d_scales": packed_dT[1],
        "gn": (np.random.uniform(0.5, 1.5, (H, 1)) * u[:, None]).astype(np.float32),
        "w1": (n((H, N)) / np.sqrt(2 * H) / u[:, None]).astype(np.float32),
        "w2": (n((K, N)) / np.sqrt(2 * K) / s).astype(np.float32),
        "offs": striped(np.random.permutation(T)[:S]),
        "k1": striped8(np.random.randint(0, G, (8, H))),
        "n1": striped(np.random.permutation(S)),
        "n2": striped(np.random.permutation(S)),
        "two": striped(np.random.permutation(T)[:S]),
        "n3": striped(np.random.permutation(S)),
    }


def reference(x_words, x_scales, d_words, d_scales, gn, w1, w2, offs, k1, n1, n2, two, n3):
    d_k1 = unpack_weight(d_words, d_scales)[np.arange(K)[:, None], runs(k1, K)]
    xq = unpack_weight(x_words, x_scales)[:, unstriped(offs)]
    h = 0.0625 * (d_k1.T @ xq)
    st = h + h[:, unstriped(n1)]
    z = f64(gn) * (st * (np.tanh(st[:, unstriped(n2)])))
    x_two = unpack_weight(x_words, x_scales)[:, unstriped(two)]
    h2 = mxq(f64(w1), 0, "e4m3").T @ mxq(z, 0, "e4m3") + mxq(f64(w2), 0, "e4m3").T @ x_two
    rl = relu(h2)
    ds = np.zeros((N, S))
    ds[:, unstriped(n3)] = rl
    return ds - (0.5 * h2)

@@ -1,0 +1,252 @@
+from contextlib import ExitStack
+
+import concourse.mybir as mybir
+
+K, T, S, N, G, H = 512, 1024, 256, 512, 2048, 512
+FLOPS = 2 * (K * H * S + H * N * S + K * N * S)
+
+F32 = mybir.dt.float32
+BF16 = mybir.dt.bfloat16
+I32 = mybir.dt.int32
+U32 = mybir.dt.uint32
+U16 = mybir.dt.uint16
+U8 = mybir.dt.uint8
+X4 = mybir.dt.float8_e4m3fn_x4
+ALU = mybir.AluOpType
+ACT = mybir.ActivationFunctionType
+
+P = 128
+PACK = 4
+HALF = S // 2
+SPARE = 16
+
+
+def tile_picked_pqmixhoppsend_none_p_kernel(tc, x_words, x_scales, d_words, d_scales, gn, w1, w2, offs, k1, n1, n2, two, n3, out):
+    nc = tc.nc
+    with ExitStack() as ctx:
+        lists = ctx.enter_context(tc.tile_pool(name="lists", bufs=1))
+        sb = ctx.enter_context(tc.tile_pool(name="sb", bufs=1))
+        shared = ctx.enter_context(tc.tile_pool(name="shared", bufs=1))
+        late = ctx.enter_context(tc.tile_pool(name="late", bufs=1))
+        ps = ctx.enter_context(tc.psum_pool(name="ps", bufs=1))
+
+        def load_list(src, name):
+            t = lists.tile(list(src.shape), U16, name=name)
+            nc.sync.dma_start(t[:], src)
+            return t
+
+        ds_win = sb.tile([P, G], U8, name="ds_win", align_bytes=64)
+        xs_win = sb.tile([P, T], U8, name="xs_win", align_bytes=64)
+
+        k1_t = load_list(k1, "k1_t")
+        ds_rows = d_scales[0].bitcast(I32)
+        for e in range(2):
+            nc.sync.dma_start(ds_win[:].bitcast(I32)[e:P:2, :], ds_rows[e:16:2, :].unsqueeze(1).to_broadcast([8, 8, G // 4]))
+        offs_t = load_list(offs, "offs_t")
+        xs_rows = x_scales[0].bitcast(I32)
+        for j in range(PACK):
+            queue = nc.sync if j < 2 else nc.gpsimd
+            queue.dma_start(xs_win[:].bitcast(I32)[j:P:4, :], xs_rows[j:16:PACK, :].unsqueeze(1).to_broadcast([4, 8, T // 4]))
+        dw_win = sb.tile([P, G], I32, name="dw_win", align_bytes=64)
+        nc.sync.dma_start(dw_win[:], d_words[0].rearrange("p n t -> p (n t)").bitcast(I32))
+        xw_win = sb.tile([P, T], I32, name="xw_win", align_bytes=64)
+        nc.sync.dma_start(xw_win[:], x_words[0].rearrange("p n t -> p (n t)").bitcast(I32))
+        two_t = load_list(two, "two_t")
+        n1_t = load_list(n1, "n1_t")
+        n2_t = load_list(n2, "n2_t")
+        n3_t = load_list(n3, "n3_t")
+        gn_t = sb.tile([P, PACK], F32, name="gn_t")
+        nc.gpsimd.dma_start(gn_t[:], gn.rearrange("(p t) o -> p (t o)", t=PACK))
+
+        h_win = [sb.tile([P, S + SPARE], F32, name="h_win%d" % t) for t in range(PACK)]
+        for t in range(PACK):
+            nc.vector.memset(h_win[t][:, S:], 0.0)
+
+        ds_g = shared.tile([P, H], U8, name="ds_g", align_bytes=64, offset=8192 - 256)
+        nc.vector.tensor_copy(ds_g[:], ds_win[:].indirect(k1_t[:]))
+        ds_d = sb.tile([P, H], U8, name="ds_d", align_bytes=64)
+        nc.vector.tensor_copy(
+            ds_d[:].rearrange("p (t c i) -> p c t i", t=PACK, i=16),
+            ds_g[:].rearrange("p (c i t) -> p c t i", t=PACK, i=16),
+        )
+        ds_d32 = ds_d[:].bitcast(I32)
+        for e in range(2):
+            nc.sync.dma_start(ds_d32[2 + e : P : 32, :], ds_d32[16 + e : P : 32, :])
+
+        w2_raw = shared.tile([P, PACK, N], F32, name="w2_raw", align_bytes=64, offset=0)
+        nc.sync.dma_start(w2_raw[:], w2.rearrange("(p j) m -> p j m", j=PACK))
+        w1_raw = shared.tile([P, PACK, N], F32, name="w1_raw", align_bytes=64, offset=8192)
+        nc.sync.dma_start(w1_raw[:], w1.rearrange("(p j) m -> p j m", j=PACK))
+
+        xq_s = sb.tile([P, S], U8, name="xq_s", align_bytes=64)
+        nc.vector.tensor_copy(xq_s[:], xs_win[:].indirect(offs_t[:]))
+        dw_g = sb.tile([P, H], U32, name="dw_g", align_bytes=64)
+        nc.vector.tensor_copy(dw_g[:], dw_win[:].bitcast(U32).indirect(k1_t[:]))
+        dw_d = sb.tile([P, H], U32, name="dw_d", align_bytes=64)
+        nc.vector.tensor_copy(
+            dw_d[:].rearrange("p (t c i) -> p c t i", t=PACK, i=4),
+            dw_g[:].rearrange("p (c i t) -> p c t i", t=PACK, i=4),
+        )
+        xq_w = sb.tile([P, S], U32, name="xq_w", align_bytes=64)
+        nc.vector.tensor_copy(xq_w[:], xw_win[:].bitcast(U32).indirect(offs_t[:]))
+
+        h_ps = [ps.tile([P, S], F32, name="h_ps%d" % t) for t in range(PACK)]
+        for t in range(PACK):
+            cols = slice(t * P, (t + 1) * P)
+            nc.tensor.matmul_mx(
+                out=h_ps[t][:], lhsT=dw_d[:, cols].bitcast(X4), lhsT_scale=ds_d[:, cols],
+                rhs=xq_w[:].bitcast(X4), rhs_scale=xq_s[:], start=True, stop=True,
+            )
+
+        x2_s = sb.tile([P, S], U8, name="x2_s", align_bytes=64)
+        nc.vector.tensor_copy(x2_s[:], xs_win[:].indirect(two_t[:]))
+        x2_w = sb.tile([P, S], U32, name="x2_w", align_bytes=64)
+        nc.vector.tensor_copy(x2_w[:], xw_win[:].bitcast(U32).indirect(two_t[:]))
+
+        def weave(dst, src, on_scalar):
+            o = dst[:].rearrange("p (c i t) -> p c t i", t=PACK, i=4)
+            s = src.rearrange("p t (c i) -> p c t i", i=4)
+            if on_scalar:
+                nc.scalar.copy(o, s)
+            else:
+                nc.vector.tensor_copy(o, s)
+
+        def quantize(src, name):
+            codes = sb.tile([P, P], U32, name=name + "_w", align_bytes=64)
+            scales = sb.tile([P, P], U8, name=name + "_s", align_bytes=64)
+            nc.vector.quantize_mx(out=codes[:].bitcast(X4), scales=scales[:], in_=src[:])
+            return codes, scales
+
+        woven = {}
+        wq = {}
+
+        def weave_w(which, b, slot=None):
+            raw = w1_raw if which == 1 else w2_raw
+            name = "wb%d_%d" % (which, b)
+            if slot is None:
+                woven[which, b] = sb.tile([P, P * PACK], BF16, name=name, align_bytes=64)
+            else:
+                woven[which, b] = late.tile([P, P * PACK], BF16, name=name, align_bytes=64, offset=1024 * slot)
+            weave(woven[which, b], raw[:, :, b * P : (b + 1) * P], slot is not None)
+
+        def quant_w(which, b):
+            wq[which, b] = quantize(woven[which, b], "wq%d_%d" % (which, b))
+
+        hop = [sb.tile([P, S], F32, name="hop%d" % t) for t in range(PACK)]
+        st = [sb.tile([P, S], F32, name="st%d" % t)[:] for t in range(PACK - 1)]
+        st_last = late.tile([P, 3 * S], F32, name="st_last", align_bytes=64, offset=0)
+        st.append(st_last[:, :S])
+        th = [sb.tile([P, S], F32, name="th%d" % t) for t in range(PACK)]
+        sg = [sb.tile([P, S], F32, name="sg%d" % t) for t in range(PACK)]
+        zf = [sb.tile([P, PACK, HALF], F32, name="zf%d" % a) for a in range(2)]
+
+        def drain_h(t):
+            nc.scalar.activation(h_win[t][:, :S], h_ps[t][:], ACT.Copy, scale=0.0625)
+
+        def fetch_h(t):
+            nc.scalar.activation(hop[t][:], h_win[t][:].indirect(n1_t[:]), ACT.Copy)
+            nc.vector.tensor_tensor(st[t], h_win[t][:, :S], hop[t][:], ALU.add)
+
+        def squash(t):
+            nc.scalar.activation(th[t][:], st[t], ACT.Tanh)
+            nc.vector.tensor_scalar(sg[t][:], st[t], gn_t[:, t : t + 1], None, ALU.mult)
+
+        def mix(t, a):
+            cols = slice(a * HALF, (a + 1) * HALF)
+            nc.vector.tensor_tensor(zf[a][:, t, :], th[t][:].indirect(n2_t[:, a * 8 : (a + 1) * 8]), sg[t][:, cols], ALU.mult)
+
+        drain_h(0)
+        drain_h(1)
+        fetch_h(0)
+        drain_h(2)
+        fetch_h(1)
+        squash(0)
+        weave_w(2, 0)
+        drain_h(3)
+        fetch_h(2)
+        squash(1)
+        mix(0, 0)
+        quant_w(2, 0)
+        weave_w(1, 0)
+        fetch_h(3)
+        squash(2)
+        mix(1, 0)
+        quant_w(1, 0)
+        squash(3)
+        mix(2, 0)
+        mix(3, 0)
+
+        zq = {}
+
+        def weave_z(a):
+            woven["z", a] = sb.tile([P, HALF * PACK], BF16, name="zb%d" % a, align_bytes=64)
+            weave(woven["z", a], zf[a][:], False)
+
+        def quant_z(a):
+            zq[a] = quantize(woven["z", a], "zq%d" % a)
+
+        o_ps = [ps.tile([P, S], F32, name="o_ps%d" % b) for b in range(PACK)]
+        ds = [sb.tile([P, S], F32, name="ds%d" % b) for b in range(PACK)]
+
+        def product(b, a):
+            cols = slice(a * HALF, (a + 1) * HALF)
+            nc.tensor.matmul_mx(
+                out=o_ps[b][:, cols], lhsT=wq[2, b][0][:].bitcast(X4), lhsT_scale=wq[2, b][1][:],
+                rhs=x2_w[:, cols].bitcast(X4), rhs_scale=x2_s[:, cols], start=True, stop=False,
+            )
+            nc.tensor.matmul_mx(
+                out=o_ps[b][:, cols], lhsT=wq[1, b][0][:].bitcast(X4), lhsT_scale=wq[1, b][1][:],
+                rhs=zq[a][0][:].bitcast(X4), rhs_scale=zq[a][1][:], start=False, stop=True,
+            )
+
+        def send(b, a):
+            cols = slice(a * HALF, (a + 1) * HALF)
+            rl = sb.tile([P, HALF], F32, name="rl%d_%d" % (b, a))
+            nc.vector.tensor_scalar(rl[:], o_ps[b][:, cols], 0.0, None, ALU.max)
+            nc.scalar.activation(ds[b][:].indirect(n3_t[:, a * 8 : (a + 1) * 8]), rl[:], ACT.Copy)
+
+        def finish(b):
+            res = sb.tile([P, S], F32, name="res%d" % b)
+            nc.vector.scalar_tensor_tensor(res[:], o_ps[b][:], -0.5, ds[b][:], ALU.mult, ALU.add)
+            nc.sync.dma_start(out[b * P : (b + 1) * P, :], res[:])
+
+        weave_w(2, 1, 0)
+        weave_w(1, 1, 1)
+        weave_w(2, 2, 2)
+        weave_z(0)
+        mix(0, 1)
+        quant_z(0)
+        product(0, 0)
+        mix(1, 1)
+        send(0, 0)
+        quant_w(2, 1)
+        quant_w(1, 1)
+        product(1, 0)
+        mix(2, 1)
+        send(1, 0)
+        mix(3, 1)
+        weave_z(1)
+        quant_z(1)
+        product(0, 1)
+        product(1, 1)
+        weave_w(1, 2)
+        send(0, 1)
+        quant_w(2, 2)
+        send(1, 1)
+        quant_w(1, 2)
+        product(2, 0)
+        weave_w(2, 3)
+        send(2, 0)
+        product(2, 1)
+        weave_w(1, 3)
+        finish(0)
+        send(2, 1)
+        quant_w(2, 3)
+        quant_w(1, 3)
+        product(3, 0)
+        finish(1)
+        send(3, 0)
+        product(3, 1)
+        send(3, 1)
+        finish(2)
+        finish(3)

@@ -28,6 +28,7 @@ def tile_picked_pqmixhoppsend_none_p_kernel(tc, x_words, x_scales, d_words, d_sc
         sb = ctx.enter_context(tc.tile_pool(name="sb", bufs=1))
         shared = ctx.enter_context(tc.tile_pool(name="shared", bufs=1))
         late = ctx.enter_context(tc.tile_pool(name="late", bufs=1))
+        tail = ctx.enter_context(tc.tile_pool(name="tail", bufs=1))
         ps = ctx.enter_context(tc.psum_pool(name="ps", bufs=1))
 
         def load_list(src, name):
@@ -40,13 +41,11 @@ def tile_picked_pqmixhoppsend_none_p_kernel(tc, x_words, x_scales, d_words, d_sc
 
         k1_t = load_list(k1, "k1_t")
         ds_rows = d_scales[0].bitcast(I32)
-        for e in range(2):
-            nc.sync.dma_start(ds_win[:].bitcast(I32)[e:P:2, :], ds_rows[e:16:2, :].unsqueeze(1).to_broadcast([8, 8, G // 4]))
+        nc.sync.dma_start(ds_win[:].bitcast(I32), ds_rows.unsqueeze(1).to_broadcast([16, 8, G // 4]))
         offs_t = load_list(offs, "offs_t")
         xs_rows = x_scales[0].bitcast(I32)
         for j in range(PACK):
-            queue = nc.sync if j < 2 else nc.gpsimd
-            queue.dma_start(xs_win[:].bitcast(I32)[j:P:4, :], xs_rows[j:16:PACK, :].unsqueeze(1).to_broadcast([4, 8, T // 4]))
+            nc.sync.dma_start(xs_win[:].bitcast(I32)[j:P:4, :], xs_rows[j:16:PACK, :].unsqueeze(1).to_broadcast([4, 8, T // 4]))
         dw_win = sb.tile([P, G], I32, name="dw_win", align_bytes=64)
         nc.sync.dma_start(dw_win[:], d_words[0].rearrange("p n t -> p (n t)").bitcast(I32))
         xw_win = sb.tile([P, T], I32, name="xw_win", align_bytes=64)
@@ -70,8 +69,8 @@ def tile_picked_pqmixhoppsend_none_p_kernel(tc, x_words, x_scales, d_words, d_sc
             ds_g[:].rearrange("p (c i t) -> p c t i", t=PACK, i=16),
         )
         ds_d32 = ds_d[:].bitcast(I32)
-        for e in range(2):
-            nc.sync.dma_start(ds_d32[2 + e : P : 32, :], ds_d32[16 + e : P : 32, :])
+        for j in range(1, PACK):
+            nc.sync.dma_start(ds_d32[j:P:32, :], ds_d32[8 * j : P : 32, :])
 
         w2_raw = shared.tile([P, PACK, N], F32, name="w2_raw", align_bytes=64, offset=0)
         nc.sync.dma_start(w2_raw[:], w2.rearrange("(p j) m -> p j m", j=PACK))
@@ -120,40 +119,47 @@ def tile_picked_pqmixhoppsend_none_p_kernel(tc, x_words, x_scales, d_words, d_sc
         woven = {}
         wq = {}
 
-        def weave_w(which, b, slot=None):
+        def weave_w(which, b, tile=None):
             raw = w1_raw if which == 1 else w2_raw
-            name = "wb%d_%d" % (which, b)
-            if slot is None:
-                woven[which, b] = sb.tile([P, P * PACK], BF16, name=name, align_bytes=64)
-            else:
-                woven[which, b] = late.tile([P, P * PACK], BF16, name=name, align_bytes=64, offset=1024 * slot)
-            weave(woven[which, b], raw[:, :, b * P : (b + 1) * P], slot is not None)
+            on_scalar = (which, b) == (1, 1)
+            if tile is None:
+                tile = sb.tile([P, P * PACK], BF16, name="wb%d_%d" % (which, b), align_bytes=64)
+            woven[which, b] = tile
+            weave(tile, raw[:, :, b * P : (b + 1) * P], on_scalar)
 
         def quant_w(which, b):
             wq[which, b] = quantize(woven[which, b], "wq%d_%d" % (which, b))
 
-        hop = [sb.tile([P, S], F32, name="hop%d" % t) for t in range(PACK)]
-        st = [sb.tile([P, S], F32, name="st%d" % t)[:] for t in range(PACK - 1)]
-        st_last = late.tile([P, 3 * S], F32, name="st_last", align_bytes=64, offset=0)
-        st.append(st_last[:, :S])
+        hop = [sb.tile([P, S], F32, name="hop%d" % t)[:] for t in range(PACK - 1)]
+        hop_last = late.tile([P, 3 * S], F32, name="hop_last", align_bytes=64, offset=0)
+        hop.append(hop_last[:, :S])
+        st = [sb.tile([P, S], F32, name="st%d" % t) for t in range(PACK)]
         th = [sb.tile([P, S], F32, name="th%d" % t) for t in range(PACK)]
-        sg = [sb.tile([P, S], F32, name="sg%d" % t) for t in range(PACK)]
+        sg = [sb.tile([P, HALF], F32, name="sg%d" % t) for t in range(PACK)]
         zf = [sb.tile([P, PACK, HALF], F32, name="zf%d" % a) for a in range(2)]
 
         def drain_h(t):
             nc.scalar.activation(h_win[t][:, :S], h_ps[t][:], ACT.Copy, scale=0.0625)
 
         def fetch_h(t):
-            nc.scalar.activation(hop[t][:], h_win[t][:].indirect(n1_t[:]), ACT.Copy)
-            nc.vector.tensor_tensor(st[t], h_win[t][:, :S], hop[t][:], ALU.add)
+            nc.scalar.activation(hop[t], h_win[t][:].indirect(n1_t[:]), ACT.Copy)
+            nc.vector.tensor_tensor(st[t][:], h_win[t][:, :S], hop[t], ALU.add)
 
         def squash(t):
-            nc.scalar.activation(th[t][:], st[t], ACT.Tanh)
-            nc.vector.tensor_scalar(sg[t][:], st[t], gn_t[:, t : t + 1], None, ALU.mult)
+            nc.scalar.activation(th[t][:], st[t][:], ACT.Tanh)
+            nc.vector.tensor_scalar(sg[t][:], st[t][:, :HALF], gn_t[:, t : t + 1], None, ALU.mult)
 
-        def mix(t, a):
-            cols = slice(a * HALF, (a + 1) * HALF)
-            nc.vector.tensor_tensor(zf[a][:, t, :], th[t][:].indirect(n2_t[:, a * 8 : (a + 1) * 8]), sg[t][:, cols], ALU.mult)
+        def mix_first(t):
+            nc.vector.tensor_tensor(zf[0][:, t, :], th[t][:].indirect(n2_t[:, 0:8]), sg[t][:], ALU.mult)
+
+        tg = {}
+
+        def fetch_second(t):
+            tg[t] = late.tile([P, HALF], F32, name="tg%d" % t, align_bytes=64, offset=1024 + 512 * t)
+            nc.scalar.activation(tg[t][:], th[t][:].indirect(n2_t[:, 8:16]), ACT.Copy)
+
+        def mix_second(t):
+            nc.vector.scalar_tensor_tensor(zf[1][:, t, :], st[t][:, HALF:], gn_t[:, t : t + 1], tg[t][:], ALU.mult, ALU.mult)
 
         drain_h(0)
         drain_h(1)
@@ -165,16 +171,18 @@ def tile_picked_pqmixhoppsend_none_p_kernel(tc, x_words, x_scales, d_words, d_sc
         drain_h(3)
         fetch_h(2)
         squash(1)
-        mix(0, 0)
+        mix_first(0)
         quant_w(2, 0)
-        weave_w(1, 0)
+        weave_w(2, 1)
         fetch_h(3)
         squash(2)
-        mix(1, 0)
-        quant_w(1, 0)
+        mix_first(1)
+        quant_w(2, 1)
+        weave_w(1, 0)
         squash(3)
-        mix(2, 0)
-        mix(3, 0)
+        mix_first(2)
+        quant_w(1, 0)
+        mix_first(3)
 
         zq = {}
 
@@ -201,52 +209,53 @@ def tile_picked_pqmixhoppsend_none_p_kernel(tc, x_words, x_scales, d_words, d_sc
 
         def send(b, a):
             cols = slice(a * HALF, (a + 1) * HALF)
-            rl = sb.tile([P, HALF], F32, name="rl%d_%d" % (b, a))
+            if (b, a) == (3, 0):
+                rl = tail.tile([P, HALF], F32, name="rl3_0", align_bytes=64, offset=2048)
+            else:
+                rl = sb.tile([P, HALF], F32, name="rl%d_%d" % (b, a))
             nc.vector.tensor_scalar(rl[:], o_ps[b][:, cols], 0.0, None, ALU.max)
             nc.scalar.activation(ds[b][:].indirect(n3_t[:, a * 8 : (a + 1) * 8]), rl[:], ACT.Copy)
 
         def finish(b):
-            res = sb.tile([P, S], F32, name="res%d" % b)
+            res = tail.tile([P, S], F32, name="res%d" % b, align_bytes=64, offset=1024 * b)
             nc.vector.scalar_tensor_tensor(res[:], o_ps[b][:], -0.5, ds[b][:], ALU.mult, ALU.add)
             nc.sync.dma_start(out[b * P : (b + 1) * P, :], res[:])
 
-        weave_w(2, 1, 0)
-        weave_w(1, 1, 1)
-        weave_w(2, 2, 2)
+        wb1_1 = late.tile([P, P * PACK], BF16, name="wb1_1", align_bytes=64, offset=0)
+        weave_w(1, 1, wb1_1)
+        for t in range(PACK):
+            fetch_second(t)
         weave_z(0)
-        mix(0, 1)
         quant_z(0)
         product(0, 0)
-        mix(1, 1)
-        send(0, 0)
-        quant_w(2, 1)
         quant_w(1, 1)
         product(1, 0)
-        mix(2, 1)
+        send(0, 0)
+        for t in range(PACK):
+            mix_second(t)
         send(1, 0)
-        mix(3, 1)
         weave_z(1)
+        weave_w(2, 2)
         quant_z(1)
         product(0, 1)
         product(1, 1)
         weave_w(1, 2)
         send(0, 1)
         quant_w(2, 2)
-        send(1, 1)
         quant_w(1, 2)
+        send(1, 1)
         product(2, 0)
         weave_w(2, 3)
         send(2, 0)
         product(2, 1)
-        weave_w(1, 3)
-        finish(0)
+        wb1_3 = tail.tile([P, P * PACK], BF16, name="wb1_3", align_bytes=64, offset=512)
+        weave_w(1, 3, wb1_3)
         send(2, 1)
         quant_w(2, 3)
         quant_w(1, 3)
         product(3, 0)
-        finish(1)
         send(3, 0)
         product(3, 1)
         send(3, 1)
-        finish(2)
-        finish(3)
+        for b in range(PACK):
+            finish(b)

@@ -19,6 +19,7 @@ P = 128
 PACK = 4
 HALF = S // 2
 SPARE = 16
+WIDE = 352
 
 
 def tile_picked_pqmixhoppsend_none_p_kernel(tc, x_words, x_scales, d_words, d_scales, gn, w1, w2, offs, k1, n1, n2, two, n3, out):
@@ -44,16 +45,25 @@ def tile_picked_pqmixhoppsend_none_p_kernel(tc, x_words, x_scales, d_words, d_sc
         nc.sync.dma_start(ds_win[:].bitcast(I32), ds_rows.unsqueeze(1).to_broadcast([16, 8, G // 4]))
         offs_t = load_list(offs, "offs_t")
         xs_rows = x_scales[0].bitcast(I32)
-        for j in range(PACK):
-            nc.sync.dma_start(xs_win[:].bitcast(I32)[j:P:4, :], xs_rows[j:16:PACK, :].unsqueeze(1).to_broadcast([4, 8, T // 4]))
-        dw_win = sb.tile([P, G], I32, name="dw_win", align_bytes=64)
+        for q in range(PACK):
+            nc.sync.dma_start(xs_win[:].bitcast(I32)[32 * q : 32 * (q + 1), :], xs_rows[PACK * q : PACK * (q + 1), :].unsqueeze(0).to_broadcast([8, PACK, T // 4]))
+        dw_win = shared.tile([P, G], I32, name="dw_win", align_bytes=64, offset=0)
         nc.sync.dma_start(dw_win[:], d_words[0].rearrange("p n t -> p (n t)").bitcast(I32))
-        xw_win = sb.tile([P, T], I32, name="xw_win", align_bytes=64)
-        nc.sync.dma_start(xw_win[:], x_words[0].rearrange("p n t -> p (n t)").bitcast(I32))
-        two_t = load_list(two, "two_t")
         n1_t = load_list(n1, "n1_t")
         n2_t = load_list(n2, "n2_t")
         n3_t = load_list(n3, "n3_t")
+        two_t = load_list(two, "two_t")
+        xw_win = sb.tile([P, T], I32, name="xw_win", align_bytes=64)
+        nc.sync.dma_start(xw_win[:], x_words[0].rearrange("p n t -> p (n t)").bitcast(I32))
+        raw = {}
+
+        def load_w(which, part, offset):
+            w = w1 if which == 1 else w2
+            raw[which, part] = shared.tile([P, PACK, N // 2], F32, name="raw%d_%d" % (which, part), align_bytes=64, offset=offset)
+            nc.sync.dma_start(raw[which, part][:], w.rearrange("(p j) m -> p j m", j=PACK)[:, :, part * 256 : (part + 1) * 256])
+
+        load_w(2, 0, 8192)
+        load_w(1, 0, 12288)
         gn_t = sb.tile([P, PACK], F32, name="gn_t")
         nc.gpsimd.dma_start(gn_t[:], gn.rearrange("(p t) o -> p (t o)", t=PACK))
 
@@ -61,7 +71,7 @@ def tile_picked_pqmixhoppsend_none_p_kernel(tc, x_words, x_scales, d_words, d_sc
         for t in range(PACK):
             nc.vector.memset(h_win[t][:, S:], 0.0)
 
-        ds_g = shared.tile([P, H], U8, name="ds_g", align_bytes=64, offset=8192 - 256)
+        ds_g = sb.tile([P, H], U8, name="ds_g", align_bytes=64)
         nc.vector.tensor_copy(ds_g[:], ds_win[:].indirect(k1_t[:]))
         ds_d = sb.tile([P, H], U8, name="ds_d", align_bytes=64)
         nc.vector.tensor_copy(
@@ -70,22 +80,20 @@ def tile_picked_pqmixhoppsend_none_p_kernel(tc, x_words, x_scales, d_words, d_sc
         )
         ds_d32 = ds_d[:].bitcast(I32)
         for j in range(1, PACK):
-            nc.sync.dma_start(ds_d32[j:P:32, :], ds_d32[8 * j : P : 32, :])
-
-        w2_raw = shared.tile([P, PACK, N], F32, name="w2_raw", align_bytes=64, offset=0)
-        nc.sync.dma_start(w2_raw[:], w2.rearrange("(p j) m -> p j m", j=PACK))
-        w1_raw = shared.tile([P, PACK, N], F32, name="w1_raw", align_bytes=64, offset=8192)
-        nc.sync.dma_start(w1_raw[:], w1.rearrange("(p j) m -> p j m", j=PACK))
+            nc.scalar.dma_start(ds_d32[j:P:32, :], ds_d32[8 * j : P : 32, :])
 
         xq_s = sb.tile([P, S], U8, name="xq_s", align_bytes=64)
         nc.vector.tensor_copy(xq_s[:], xs_win[:].indirect(offs_t[:]))
         dw_g = sb.tile([P, H], U32, name="dw_g", align_bytes=64)
         nc.vector.tensor_copy(dw_g[:], dw_win[:].bitcast(U32).indirect(k1_t[:]))
+        load_w(2, 1, 0)
+        load_w(1, 1, 4096)
         dw_d = sb.tile([P, H], U32, name="dw_d", align_bytes=64)
         nc.vector.tensor_copy(
             dw_d[:].rearrange("p (t c i) -> p c t i", t=PACK, i=4),
             dw_g[:].rearrange("p (c i t) -> p c t i", t=PACK, i=4),
         )
+
         xq_w = sb.tile([P, S], U32, name="xq_w", align_bytes=64)
         nc.vector.tensor_copy(xq_w[:], xw_win[:].bitcast(U32).indirect(offs_t[:]))
 
@@ -99,47 +107,49 @@ def tile_picked_pqmixhoppsend_none_p_kernel(tc, x_words, x_scales, d_words, d_sc
 
         x2_s = sb.tile([P, S], U8, name="x2_s", align_bytes=64)
         nc.vector.tensor_copy(x2_s[:], xs_win[:].indirect(two_t[:]))
-        x2_w = sb.tile([P, S], U32, name="x2_w", align_bytes=64)
-        nc.vector.tensor_copy(x2_w[:], xw_win[:].bitcast(U32).indirect(two_t[:]))
 
         def weave(dst, src, on_scalar):
-            o = dst[:].rearrange("p (c i t) -> p c t i", t=PACK, i=4)
+            o = dst.rearrange("p (c i t) -> p c t i", t=PACK, i=4)
             s = src.rearrange("p t (c i) -> p c t i", i=4)
             if on_scalar:
                 nc.scalar.copy(o, s)
             else:
                 nc.vector.tensor_copy(o, s)
 
-        def quantize(src, name):
-            codes = sb.tile([P, P], U32, name=name + "_w", align_bytes=64)
-            scales = sb.tile([P, P], U8, name=name + "_s", align_bytes=64)
-            nc.vector.quantize_mx(out=codes[:].bitcast(X4), scales=scales[:], in_=src[:])
-            return codes, scales
+        def w_block(which, b):
+            return raw[which, b // 2][:, :, (b % 2) * P : (b % 2 + 1) * P]
 
-        woven = {}
-        wq = {}
+        def quantize(codes, scales, src):
+            nc.vector.quantize_mx(out=codes.bitcast(X4), scales=scales, in_=src)
 
-        def weave_w(which, b, tile=None):
-            raw = w1_raw if which == 1 else w2_raw
-            on_scalar = (which, b) == (1, 1)
-            if tile is None:
-                tile = sb.tile([P, P * PACK], BF16, name="wb%d_%d" % (which, b), align_bytes=64)
-            woven[which, b] = tile
-            weave(tile, raw[:, :, b * P : (b + 1) * P], on_scalar)
+        wq_w = [sb.tile([P, 2 * P], U32, name="wq_w%d" % b, align_bytes=64) for b in range(PACK)]
+        wq_s = [sb.tile([P, 2 * P], U8, name="wq_s%d" % b, align_bytes=64) for b in range(PACK)]
+        wb = [sb.tile([P, 2, P * PACK], BF16, name="wb%d" % b, align_bytes=64) for b in range(2)]
 
-        def quant_w(which, b):
-            wq[which, b] = quantize(woven[which, b], "wq%d_%d" % (which, b))
+        def weave_w(which, b, on_scalar=False):
+            weave(wb[b][:, which % 2, :], w_block(which, b), on_scalar)
+
+        def quant_w(b):
+            quantize(wq_w[b][:], wq_s[b][:], wb[b][:].rearrange("p a c -> p (a c)"))
+
+        weave_w(2, 0, True)
+        weave_w(2, 1, True)
 
         hop = [sb.tile([P, S], F32, name="hop%d" % t)[:] for t in range(PACK - 1)]
-        hop_last = late.tile([P, 3 * S], F32, name="hop_last", align_bytes=64, offset=0)
-        hop.append(hop_last[:, :S])
+        hop_3 = late.tile([P, 2 * S], F32, name="hop_3", align_bytes=64, offset=0)
+        hop.append(hop_3[:, :S])
         st = [sb.tile([P, S], F32, name="st%d" % t) for t in range(PACK)]
         th = [sb.tile([P, S], F32, name="th%d" % t) for t in range(PACK)]
         sg = [sb.tile([P, HALF], F32, name="sg%d" % t) for t in range(PACK)]
-        zf = [sb.tile([P, PACK, HALF], F32, name="zf%d" % a) for a in range(2)]
+        zf_wide = tail.tile([P, 2 * PACK, HALF], F32, name="zf_wide", align_bytes=64, offset=0)
+        zf = [zf_wide[:, :PACK, :], sb.tile([P, PACK, HALF], F32, name="zf1")[:]]
+        first, second, both = slice(0, HALF), slice(HALF, S), slice(0, S)
 
         def drain_h(t):
-            nc.scalar.activation(h_win[t][:, :S], h_ps[t][:], ACT.Copy, scale=0.0625)
+            if t in (0, 3):
+                nc.scalar.activation(h_win[t][:, :S], h_ps[t][:], ACT.Copy, scale=0.0625)
+            else:
+                nc.vector.tensor_scalar(h_win[t][:, :S], h_ps[t][:], 0.0625, None, ALU.mult)
 
         def fetch_h(t):
             nc.scalar.activation(hop[t], h_win[t][:].indirect(n1_t[:]), ACT.Copy)
@@ -147,115 +157,87 @@ def tile_picked_pqmixhoppsend_none_p_kernel(tc, x_words, x_scales, d_words, d_sc
 
         def squash(t):
             nc.scalar.activation(th[t][:], st[t][:], ACT.Tanh)
-            nc.vector.tensor_scalar(sg[t][:], st[t][:, :HALF], gn_t[:, t : t + 1], None, ALU.mult)
+            nc.vector.tensor_scalar(sg[t][:], st[t][:, first], gn_t[:, t : t + 1], None, ALU.mult)
 
         def mix_first(t):
             nc.vector.tensor_tensor(zf[0][:, t, :], th[t][:].indirect(n2_t[:, 0:8]), sg[t][:], ALU.mult)
 
-        tg = {}
-
-        def fetch_second(t):
-            tg[t] = late.tile([P, HALF], F32, name="tg%d" % t, align_bytes=64, offset=1024 + 512 * t)
-            nc.scalar.activation(tg[t][:], th[t][:].indirect(n2_t[:, 8:16]), ACT.Copy)
-
-        def mix_second(t):
-            nc.vector.scalar_tensor_tensor(zf[1][:, t, :], st[t][:, HALF:], gn_t[:, t : t + 1], tg[t][:], ALU.mult, ALU.mult)
-
-        drain_h(0)
-        drain_h(1)
+        for t in range(3):
+            drain_h(t)
+        x2_w = sb.tile([P, S], U32, name="x2_w", align_bytes=64)
+        nc.vector.tensor_copy(x2_w[:], xw_win[:].bitcast(U32).indirect(two_t[:]))
         fetch_h(0)
-        drain_h(2)
         fetch_h(1)
         squash(0)
-        weave_w(2, 0)
         drain_h(3)
+        weave_w(1, 0)
         fetch_h(2)
         squash(1)
         mix_first(0)
-        quant_w(2, 0)
-        weave_w(2, 1)
+        quant_w(0)
         fetch_h(3)
         squash(2)
         mix_first(1)
-        quant_w(2, 1)
-        weave_w(1, 0)
+        weave_w(1, 1)
         squash(3)
         mix_first(2)
-        quant_w(1, 0)
         mix_first(3)
 
-        zq = {}
-
-        def weave_z(a):
-            woven["z", a] = sb.tile([P, HALF * PACK], BF16, name="zb%d" % a, align_bytes=64)
-            weave(woven["z", a], zf[a][:], False)
+        o_ps = [ps.tile([P, S], F32, name="o_ps%d" % b) for b in range(PACK)]
+        ds = [sb.tile([P, S if b < 2 else WIDE], F32, name="ds%d" % b) for b in range(PACK)]
+        zq_w = sb.tile([P, S], U32, name="zq_w", align_bytes=64)
+        zq_s = sb.tile([P, S], U8, name="zq_s", align_bytes=64)
 
         def quant_z(a):
-            zq[a] = quantize(woven["z", a], "zq%d" % a)
+            cols = first if a == 0 else second
+            zb = sb.tile([P, HALF * PACK], BF16, name="zb%d" % a, align_bytes=64)
+            weave(zb[:], zf[a], False)
+            quantize(zq_w[:, cols], zq_s[:, cols], zb[:])
+            return zb
 
-        o_ps = [ps.tile([P, S], F32, name="o_ps%d" % b) for b in range(PACK)]
-        ds = [sb.tile([P, S], F32, name="ds%d" % b) for b in range(PACK)]
-
-        def product(b, a):
-            cols = slice(a * HALF, (a + 1) * HALF)
+        def product(b, cols):
             nc.tensor.matmul_mx(
-                out=o_ps[b][:, cols], lhsT=wq[2, b][0][:].bitcast(X4), lhsT_scale=wq[2, b][1][:],
+                out=o_ps[b][:, cols], lhsT=wq_w[b][:, :P].bitcast(X4), lhsT_scale=wq_s[b][:, :P],
                 rhs=x2_w[:, cols].bitcast(X4), rhs_scale=x2_s[:, cols], start=True, stop=False,
             )
             nc.tensor.matmul_mx(
-                out=o_ps[b][:, cols], lhsT=wq[1, b][0][:].bitcast(X4), lhsT_scale=wq[1, b][1][:],
-                rhs=zq[a][0][:].bitcast(X4), rhs_scale=zq[a][1][:], start=False, stop=True,
+                out=o_ps[b][:, cols], lhsT=wq_w[b][:, P:].bitcast(X4), lhsT_scale=wq_s[b][:, P:],
+                rhs=zq_w[:, cols].bitcast(X4), rhs_scale=zq_s[:, cols], start=False, stop=True,
             )
 
-        def send(b, a):
-            cols = slice(a * HALF, (a + 1) * HALF)
-            if (b, a) == (3, 0):
-                rl = tail.tile([P, HALF], F32, name="rl3_0", align_bytes=64, offset=2048)
-            else:
-                rl = sb.tile([P, HALF], F32, name="rl%d_%d" % (b, a))
+        def send(b, cols):
+            rl = sb.tile([P, cols.stop - cols.start], F32, name="rl%d_%d" % (b, cols.start))
             nc.vector.tensor_scalar(rl[:], o_ps[b][:, cols], 0.0, None, ALU.max)
-            nc.scalar.activation(ds[b][:].indirect(n3_t[:, a * 8 : (a + 1) * 8]), rl[:], ACT.Copy)
+            nc.scalar.activation(ds[b][:].indirect(n3_t[:, cols.start // 16 : cols.stop // 16]), rl[:], ACT.Copy)
 
         def finish(b):
             res = tail.tile([P, S], F32, name="res%d" % b, align_bytes=64, offset=1024 * b)
-            nc.vector.scalar_tensor_tensor(res[:], o_ps[b][:], -0.5, ds[b][:], ALU.mult, ALU.add)
+            nc.vector.scalar_tensor_tensor(res[:], o_ps[b][:], -0.5, ds[b][:, :S], ALU.mult, ALU.add)
             nc.sync.dma_start(out[b * P : (b + 1) * P, :], res[:])
 
-        wb1_1 = late.tile([P, P * PACK], BF16, name="wb1_1", align_bytes=64, offset=0)
-        weave_w(1, 1, wb1_1)
+        far = late.tile([P, PACK, HALF], F32, name="far", align_bytes=64, offset=0)
         for t in range(PACK):
-            fetch_second(t)
-        weave_z(0)
-        quant_z(0)
-        product(0, 0)
-        quant_w(1, 1)
-        product(1, 0)
-        send(0, 0)
+            nc.scalar.activation(far[:, t, :], th[t][:].indirect(n2_t[:, 8:16]), ACT.Copy)
+        zb0 = quant_z(0)
+        product(0, first)
+        quant_w(1)
+        product(1, first)
+        send(0, first)
         for t in range(PACK):
-            mix_second(t)
-        send(1, 0)
-        weave_z(1)
-        weave_w(2, 2)
-        quant_z(1)
-        product(0, 1)
-        product(1, 1)
-        weave_w(1, 2)
-        send(0, 1)
-        quant_w(2, 2)
-        quant_w(1, 2)
-        send(1, 1)
-        product(2, 0)
-        weave_w(2, 3)
-        send(2, 0)
-        product(2, 1)
-        wb1_3 = tail.tile([P, P * PACK], BF16, name="wb1_3", align_bytes=64, offset=512)
-        weave_w(1, 3, wb1_3)
-        send(2, 1)
-        quant_w(2, 3)
-        quant_w(1, 3)
-        product(3, 0)
-        send(3, 0)
-        product(3, 1)
-        send(3, 1)
+            nc.vector.scalar_tensor_tensor(zf[1][:, t, :], st[t][:, second], gn_t[:, t : t + 1], far[:, t, :], ALU.mult, ALU.mult)
+        send(1, first)
+        zb1 = quant_z(1)
+        product(0, second)
+        send(0, second)
+        product(1, second)
+        send(1, second)
+        wb.append(tail.tile([P, 2, P * PACK], BF16, name="wb2", align_bytes=64, offset=2048))
+        wb.append(tail.tile([P, 2, P * PACK], BF16, name="wb3", align_bytes=64, offset=0))
+        for b in (2, 3):
+            weave_w(2, b)
+            weave_w(1, b)
+            quant_w(b)
+            product(b, both)
+            send(b, both)
         for b in range(PACK):
             finish(b)

@@ -47,14 +47,14 @@ def tile_picked_pqmixhoppsend_none_p_kernel(tc, x_words, x_scales, d_words, d_sc
         xs_rows = x_scales[0].bitcast(I32)
         for q in range(PACK):
             nc.sync.dma_start(xs_win[:].bitcast(I32)[32 * q : 32 * (q + 1), :], xs_rows[PACK * q : PACK * (q + 1), :].unsqueeze(0).to_broadcast([8, PACK, T // 4]))
-        dw_win = shared.tile([P, G], I32, name="dw_win", align_bytes=64, offset=0)
+        dw_win = sb.tile([P, G], I32, name="dw_win", align_bytes=64)
         nc.sync.dma_start(dw_win[:], d_words[0].rearrange("p n t -> p (n t)").bitcast(I32))
+        xw_win = sb.tile([P, T], I32, name="xw_win", align_bytes=64)
+        nc.sync.dma_start(xw_win[:], x_words[0].rearrange("p n t -> p (n t)").bitcast(I32))
+        two_t = load_list(two, "two_t")
         n1_t = load_list(n1, "n1_t")
         n2_t = load_list(n2, "n2_t")
         n3_t = load_list(n3, "n3_t")
-        two_t = load_list(two, "two_t")
-        xw_win = sb.tile([P, T], I32, name="xw_win", align_bytes=64)
-        nc.sync.dma_start(xw_win[:], x_words[0].rearrange("p n t -> p (n t)").bitcast(I32))
         raw = {}
 
         def load_w(which, part, offset):
@@ -62,8 +62,6 @@ def tile_picked_pqmixhoppsend_none_p_kernel(tc, x_words, x_scales, d_words, d_sc
             raw[which, part] = shared.tile([P, PACK, N // 2], F32, name="raw%d_%d" % (which, part), align_bytes=64, offset=offset)
             nc.sync.dma_start(raw[which, part][:], w.rearrange("(p j) m -> p j m", j=PACK)[:, :, part * 256 : (part + 1) * 256])
 
-        load_w(2, 0, 8192)
-        load_w(1, 0, 12288)
         gn_t = sb.tile([P, PACK], F32, name="gn_t")
         nc.gpsimd.dma_start(gn_t[:], gn.rearrange("(p t) o -> p (t o)", t=PACK))
 
@@ -71,23 +69,26 @@ def tile_picked_pqmixhoppsend_none_p_kernel(tc, x_words, x_scales, d_words, d_sc
         for t in range(PACK):
             nc.vector.memset(h_win[t][:, S:], 0.0)
 
-        ds_g = sb.tile([P, H], U8, name="ds_g", align_bytes=64)
-        nc.vector.tensor_copy(ds_g[:], ds_win[:].indirect(k1_t[:]))
+        ds_wide = shared.tile([P, 16384], U8, name="ds_wide", align_bytes=64, offset=0)
+        ds_g = ds_wide[:, :H]
+        nc.vector.tensor_copy(ds_g, ds_win[:].indirect(k1_t[:]))
         ds_d = sb.tile([P, H], U8, name="ds_d", align_bytes=64)
         nc.vector.tensor_copy(
             ds_d[:].rearrange("p (t c i) -> p c t i", t=PACK, i=16),
-            ds_g[:].rearrange("p (c i t) -> p c t i", t=PACK, i=16),
+            ds_g.rearrange("p (c i t) -> p c t i", t=PACK, i=16),
         )
         ds_d32 = ds_d[:].bitcast(I32)
         for j in range(1, PACK):
-            nc.scalar.dma_start(ds_d32[j:P:32, :], ds_d32[8 * j : P : 32, :])
+            nc.sync.dma_start(ds_d32[j:P:32, :], ds_d32[8 * j : P : 32, :])
+        load_w(2, 0, 12288)
+        load_w(1, 0, 0)
+        load_w(2, 1, 4096)
+        load_w(1, 1, 8192)
 
         xq_s = sb.tile([P, S], U8, name="xq_s", align_bytes=64)
         nc.vector.tensor_copy(xq_s[:], xs_win[:].indirect(offs_t[:]))
         dw_g = sb.tile([P, H], U32, name="dw_g", align_bytes=64)
         nc.vector.tensor_copy(dw_g[:], dw_win[:].bitcast(U32).indirect(k1_t[:]))
-        load_w(2, 1, 0)
-        load_w(1, 1, 4096)
         dw_d = sb.tile([P, H], U32, name="dw_d", align_bytes=64)
         nc.vector.tensor_copy(
             dw_d[:].rearrange("p (t c i) -> p c t i", t=PACK, i=4),
@@ -124,7 +125,7 @@ def tile_picked_pqmixhoppsend_none_p_kernel(tc, x_words, x_scales, d_words, d_sc
 
         wq_w = [sb.tile([P, 2 * P], U32, name="wq_w%d" % b, align_bytes=64) for b in range(PACK)]
         wq_s = [sb.tile([P, 2 * P], U8, name="wq_s%d" % b, align_bytes=64) for b in range(PACK)]
-        wb = [sb.tile([P, 2, P * PACK], BF16, name="wb%d" % b, align_bytes=64) for b in range(2)]
+        wb = [sb.tile([P, 2, P * PACK], BF16, name="wb0", align_bytes=64)]
 
         def weave_w(which, b, on_scalar=False):
             weave(wb[b][:, which % 2, :], w_block(which, b), on_scalar)
@@ -132,11 +133,8 @@ def tile_picked_pqmixhoppsend_none_p_kernel(tc, x_words, x_scales, d_words, d_sc
         def quant_w(b):
             quantize(wq_w[b][:], wq_s[b][:], wb[b][:].rearrange("p a c -> p (a c)"))
 
-        weave_w(2, 0, True)
-        weave_w(2, 1, True)
-
         hop = [sb.tile([P, S], F32, name="hop%d" % t)[:] for t in range(PACK - 1)]
-        hop_3 = late.tile([P, 2 * S], F32, name="hop_3", align_bytes=64, offset=0)
+        hop_3 = late.tile([P, 4 * S], F32, name="hop_3", align_bytes=64, offset=0)
         hop.append(hop_3[:, :S])
         st = [sb.tile([P, S], F32, name="st%d" % t) for t in range(PACK)]
         th = [sb.tile([P, S], F32, name="th%d" % t) for t in range(PACK)]
@@ -146,7 +144,7 @@ def tile_picked_pqmixhoppsend_none_p_kernel(tc, x_words, x_scales, d_words, d_sc
         first, second, both = slice(0, HALF), slice(HALF, S), slice(0, S)
 
         def drain_h(t):
-            if t in (0, 3):
+            if t != 2:
                 nc.scalar.activation(h_win[t][:, :S], h_ps[t][:], ACT.Copy, scale=0.0625)
             else:
                 nc.vector.tensor_scalar(h_win[t][:, :S], h_ps[t][:], 0.0625, None, ALU.mult)
@@ -167,6 +165,7 @@ def tile_picked_pqmixhoppsend_none_p_kernel(tc, x_words, x_scales, d_words, d_sc
         x2_w = sb.tile([P, S], U32, name="x2_w", align_bytes=64)
         nc.vector.tensor_copy(x2_w[:], xw_win[:].bitcast(U32).indirect(two_t[:]))
         fetch_h(0)
+        weave_w(2, 0)
         fetch_h(1)
         squash(0)
         drain_h(3)
@@ -178,7 +177,6 @@ def tile_picked_pqmixhoppsend_none_p_kernel(tc, x_words, x_scales, d_words, d_sc
         fetch_h(3)
         squash(2)
         mix_first(1)
-        weave_w(1, 1)
         squash(3)
         mix_first(2)
         mix_first(3)
@@ -218,11 +216,14 @@ def tile_picked_pqmixhoppsend_none_p_kernel(tc, x_words, x_scales, d_words, d_sc
         far = late.tile([P, PACK, HALF], F32, name="far", align_bytes=64, offset=0)
         for t in range(PACK):
             nc.scalar.activation(far[:, t, :], th[t][:].indirect(n2_t[:, 8:16]), ACT.Copy)
+        wb.append(late.tile([P, 2, P * PACK], BF16, name="wb1", align_bytes=64, offset=2048))
+        weave_w(2, 1, True)
         zb0 = quant_z(0)
         product(0, first)
+        send(0, first)
+        weave_w(1, 1)
         quant_w(1)
         product(1, first)
-        send(0, first)
         for t in range(PACK):
             nc.vector.scalar_tensor_tensor(zf[1][:, t, :], st[t][:, second], gn_t[:, t : t + 1], far[:, t, :], ALU.mult, ALU.mult)
         send(1, first)

from contextlib import ExitStack

import concourse.mybir as mybir

K, T, S, N, G, H = 512, 1024, 256, 512, 2048, 512
FLOPS = 2 * (K * H * S + H * N * S + K * N * S)

F32 = mybir.dt.float32
BF16 = mybir.dt.bfloat16
I32 = mybir.dt.int32
U32 = mybir.dt.uint32
U16 = mybir.dt.uint16
U8 = mybir.dt.uint8
X4 = mybir.dt.float8_e4m3fn_x4
ALU = mybir.AluOpType
ACT = mybir.ActivationFunctionType

P = 128
PACK = 4
HALF = S // 2
SPARE = 16
WIDE = 352


def tile_picked_pqmixhoppsend_none_p_kernel(tc, x_words, x_scales, d_words, d_scales, gn, w1, w2, offs, k1, n1, n2, two, n3, out):
    nc = tc.nc
    with ExitStack() as ctx:
        lists = ctx.enter_context(tc.tile_pool(name="lists", bufs=1))
        sb = ctx.enter_context(tc.tile_pool(name="sb", bufs=1))
        shared = ctx.enter_context(tc.tile_pool(name="shared", bufs=1))
        late = ctx.enter_context(tc.tile_pool(name="late", bufs=1))
        tail = ctx.enter_context(tc.tile_pool(name="tail", bufs=1))
        ps = ctx.enter_context(tc.psum_pool(name="ps", bufs=1))

        def load_list(src, name):
            t = lists.tile(list(src.shape), U16, name=name)
            nc.sync.dma_start(t[:], src)
            return t

        ds_win = sb.tile([P, G], U8, name="ds_win", align_bytes=64)
        xs_win = sb.tile([P, T], U8, name="xs_win", align_bytes=64)

        k1_t = load_list(k1, "k1_t")
        ds_rows = d_scales[0].bitcast(I32)
        nc.sync.dma_start(ds_win[:].bitcast(I32), ds_rows.unsqueeze(1).to_broadcast([16, 8, G // 4]))
        offs_t = load_list(offs, "offs_t")
        xs_rows = x_scales[0].bitcast(I32)
        for q in range(PACK):
            nc.sync.dma_start(xs_win[:].bitcast(I32)[32 * q : 32 * (q + 1), :], xs_rows[PACK * q : PACK * (q + 1), :].unsqueeze(0).to_broadcast([8, PACK, T // 4]))
        dw_win = sb.tile([P, G], I32, name="dw_win", align_bytes=64)
        nc.sync.dma_start(dw_win[:], d_words[0].rearrange("p n t -> p (n t)").bitcast(I32))
        xw_win = sb.tile([P, T], I32, name="xw_win", align_bytes=64)
        nc.sync.dma_start(xw_win[:], x_words[0].rearrange("p n t -> p (n t)").bitcast(I32))
        two_t = load_list(two, "two_t")
        n1_t = load_list(n1, "n1_t")
        n2_t = load_list(n2, "n2_t")
        n3_t = load_list(n3, "n3_t")
        raw = {}

        def load_w(which, part, offset):
            w = w1 if which == 1 else w2
            raw[which, part] = shared.tile([P, PACK, N // 2], F32, name="raw%d_%d" % (which, part), align_bytes=64, offset=offset)
            nc.sync.dma_start(raw[which, part][:], w.rearrange("(p j) m -> p j m", j=PACK)[:, :, part * 256 : (part + 1) * 256])

        gn_t = sb.tile([P, PACK], F32, name="gn_t")
        nc.gpsimd.dma_start(gn_t[:], gn.rearrange("(p t) o -> p (t o)", t=PACK))

        h_win = [sb.tile([P, S + SPARE], F32, name="h_win%d" % t) for t in range(PACK)]
        for t in range(PACK):
            nc.vector.memset(h_win[t][:, S:], 0.0)

        ds_wide = shared.tile([P, 16384], U8, name="ds_wide", align_bytes=64, offset=0)
        ds_g = ds_wide[:, :H]
        nc.vector.tensor_copy(ds_g, ds_win[:].indirect(k1_t[:]))
        ds_d = sb.tile([P, H], U8, name="ds_d", align_bytes=64)
        nc.vector.tensor_copy(
            ds_d[:].rearrange("p (t c i) -> p c t i", t=PACK, i=16),
            ds_g.rearrange("p (c i t) -> p c t i", t=PACK, i=16),
        )
        ds_d32 = ds_d[:].bitcast(I32)
        for j in range(1, PACK):
            nc.sync.dma_start(ds_d32[j:P:32, :], ds_d32[8 * j : P : 32, :])
        load_w(2, 0, 12288)
        load_w(1, 0, 0)
        load_w(2, 1, 4096)
        load_w(1, 1, 8192)

        xq_s = sb.tile([P, S], U8, name="xq_s", align_bytes=64)
        nc.vector.tensor_copy(xq_s[:], xs_win[:].indirect(offs_t[:]))
        dw_g = sb.tile([P, H], U32, name="dw_g", align_bytes=64)
        nc.vector.tensor_copy(dw_g[:], dw_win[:].bitcast(U32).indirect(k1_t[:]))
        dw_d = sb.tile([P, H], U32, name="dw_d", align_bytes=64)
        nc.vector.tensor_copy(
            dw_d[:].rearrange("p (t c i) -> p c t i", t=PACK, i=4),
            dw_g[:].rearrange("p (c i t) -> p c t i", t=PACK, i=4),
        )

        xq_w = sb.tile([P, S], U32, name="xq_w", align_bytes=64)
        nc.vector.tensor_copy(xq_w[:], xw_win[:].bitcast(U32).indirect(offs_t[:]))

        h_ps = [ps.tile([P, S], F32, name="h_ps%d" % t) for t in range(PACK)]
        for t in range(PACK):
            cols = slice(t * P, (t + 1) * P)
            nc.tensor.matmul_mx(
                out=h_ps[t][:], lhsT=dw_d[:, cols].bitcast(X4), lhsT_scale=ds_d[:, cols],
                rhs=xq_w[:].bitcast(X4), rhs_scale=xq_s[:], start=True, stop=True,
            )

        x2_s = sb.tile([P, S], U8, name="x2_s", align_bytes=64)
        nc.vector.tensor_copy(x2_s[:], xs_win[:].indirect(two_t[:]))

        def weave(dst, src, on_scalar):
            o = dst.rearrange("p (c i t) -> p c t i", t=PACK, i=4)
            s = src.rearrange("p t (c i) -> p c t i", i=4)
            if on_scalar:
                nc.scalar.copy(o, s)
            else:
                nc.vector.tensor_copy(o, s)

        def w_block(which, b):
            return raw[which, b // 2][:, :, (b % 2) * P : (b % 2 + 1) * P]

        def quantize(codes, scales, src):
            nc.vector.quantize_mx(out=codes.bitcast(X4), scales=scales, in_=src)

        wq_w = [sb.tile([P, 2 * P], U32, name="wq_w%d" % b, align_bytes=64) for b in range(PACK)]
        wq_s = [sb.tile([P, 2 * P], U8, name="wq_s%d" % b, align_bytes=64) for b in range(PACK)]
        wb = [sb.tile([P, 2, P * PACK], BF16, name="wb0", align_bytes=64)]

        def weave_w(which, b, on_scalar=False):
            weave(wb[b][:, which % 2, :], w_block(which, b), on_scalar)

        def quant_w(b):
            quantize(wq_w[b][:], wq_s[b][:], wb[b][:].rearrange("p a c -> p (a c)"))

        hop = [sb.tile([P, S], F32, name="hop%d" % t)[:] for t in range(PACK - 1)]
        hop_3 = late.tile([P, 4 * S], F32, name="hop_3", align_bytes=64, offset=0)
        hop.append(hop_3[:, :S])
        st = [sb.tile([P, S], F32, name="st%d" % t) for t in range(PACK)]
        th = [sb.tile([P, S], F32, name="th%d" % t) for t in range(PACK)]
        sg = [sb.tile([P, HALF], F32, name="sg%d" % t) for t in range(PACK)]
        zf_wide = tail.tile([P, 2 * PACK, HALF], F32, name="zf_wide", align_bytes=64, offset=0)
        zf = [zf_wide[:, :PACK, :], sb.tile([P, PACK, HALF], F32, name="zf1")[:]]
        first, second, both = slice(0, HALF), slice(HALF, S), slice(0, S)

        def drain_h(t):
            if t != 2:
                nc.scalar.activation(h_win[t][:, :S], h_ps[t][:], ACT.Copy, scale=0.0625)
            else:
                nc.vector.tensor_scalar(h_win[t][:, :S], h_ps[t][:], 0.0625, None, ALU.mult)

        def fetch_h(t):
            nc.scalar.activation(hop[t], h_win[t][:].indirect(n1_t[:]), ACT.Copy)
            nc.vector.tensor_tensor(st[t][:], h_win[t][:, :S], hop[t], ALU.add)

        def squash(t):
            nc.scalar.activation(th[t][:], st[t][:], ACT.Tanh)
            nc.vector.tensor_scalar(sg[t][:], st[t][:, first], gn_t[:, t : t + 1], None, ALU.mult)

        def mix_first(t):
            nc.vector.tensor_tensor(zf[0][:, t, :], th[t][:].indirect(n2_t[:, 0:8]), sg[t][:], ALU.mult)

        for t in range(3):
            drain_h(t)
        x2_w = sb.tile([P, S], U32, name="x2_w", align_bytes=64)
        nc.vector.tensor_copy(x2_w[:], xw_win[:].bitcast(U32).indirect(two_t[:]))
        fetch_h(0)
        weave_w(2, 0)
        fetch_h(1)
        squash(0)
        drain_h(3)
        weave_w(1, 0)
        fetch_h(2)
        squash(1)
        mix_first(0)
        quant_w(0)
        fetch_h(3)
        squash(2)
        mix_first(1)
        squash(3)
        mix_first(2)
        mix_first(3)

        o_ps = [ps.tile([P, S], F32, name="o_ps%d" % b) for b in range(PACK)]
        ds = [sb.tile([P, S if b < 2 else WIDE], F32, name="ds%d" % b) for b in range(PACK)]
        zq_w = sb.tile([P, S], U32, name="zq_w", align_bytes=64)
        zq_s = sb.tile([P, S], U8, name="zq_s", align_bytes=64)

        def quant_z(a):
            cols = first if a == 0 else second
            zb = sb.tile([P, HALF * PACK], BF16, name="zb%d" % a, align_bytes=64)
            weave(zb[:], zf[a], False)
            quantize(zq_w[:, cols], zq_s[:, cols], zb[:])
            return zb

        def product(b, cols):
            nc.tensor.matmul_mx(
                out=o_ps[b][:, cols], lhsT=wq_w[b][:, :P].bitcast(X4), lhsT_scale=wq_s[b][:, :P],
                rhs=x2_w[:, cols].bitcast(X4), rhs_scale=x2_s[:, cols], start=True, stop=False,
            )
            nc.tensor.matmul_mx(
                out=o_ps[b][:, cols], lhsT=wq_w[b][:, P:].bitcast(X4), lhsT_scale=wq_s[b][:, P:],
                rhs=zq_w[:, cols].bitcast(X4), rhs_scale=zq_s[:, cols], start=False, stop=True,
            )

        def send(b, cols):
            rl = sb.tile([P, cols.stop - cols.start], F32, name="rl%d_%d" % (b, cols.start))
            nc.vector.tensor_scalar(rl[:], o_ps[b][:, cols], 0.0, None, ALU.max)
            nc.scalar.activation(ds[b][:].indirect(n3_t[:, cols.start // 16 : cols.stop // 16]), rl[:], ACT.Copy)

        def finish(b):
            res = tail.tile([P, S], F32, name="res%d" % b, align_bytes=64, offset=1024 * b)
            nc.vector.scalar_tensor_tensor(res[:], o_ps[b][:], -0.5, ds[b][:, :S], ALU.mult, ALU.add)
            nc.sync.dma_start(out[b * P : (b + 1) * P, :], res[:])

        far = late.tile([P, PACK, HALF], F32, name="far", align_bytes=64, offset=0)
        for t in range(PACK):
            nc.scalar.activation(far[:, t, :], th[t][:].indirect(n2_t[:, 8:16]), ACT.Copy)
        wb.append(late.tile([P, 2, P * PACK], BF16, name="wb1", align_bytes=64, offset=2048))
        weave_w(2, 1, True)
        zb0 = quant_z(0)
        product(0, first)
        send(0, first)
        weave_w(1, 1)
        quant_w(1)
        product(1, first)
        for t in range(PACK):
            nc.vector.scalar_tensor_tensor(zf[1][:, t, :], st[t][:, second], gn_t[:, t : t + 1], far[:, t, :], ALU.mult, ALU.mult)
        send(1, first)
        zb1 = quant_z(1)
        product(0, second)
        send(0, second)
        product(1, second)
        send(1, second)
        wb.append(tail.tile([P, 2, P * PACK], BF16, name="wb2", align_bytes=64, offset=2048))
        wb.append(tail.tile([P, 2, P * PACK], BF16, name="wb3", align_bytes=64, offset=0))
        for b in (2, 3):
            weave_w(2, b)
            weave_w(1, b)
            quant_w(b)
            product(b, both)
            send(b, both)
        for b in range(PACK):
            finish(b)
